import numpy as np, ml_dtypes
CORES = [21,85,149,213,277,341,405,469]
N = 8
TK, NT = 256, 4
def setup_inputs(rng):
    x = rng.standard_normal((NT, 128, TK), dtype=np.float32).astype(ml_dtypes.bfloat16)
    return {"x": np.broadcast_to(x, (2, NT, 128, TK)).reshape(N, 128, TK).copy(), "w": rng.standard_normal((N, 128, NT * 128), dtype=np.float32).astype(ml_dtypes.bfloat16)}
def setup_inputs_big(rng):
    d = setup_inputs(rng)
    for k in ("x", "w"): d[k] = (d[k].astype(np.float32) * 1024.0).astype(d[k].dtype)
    return d
def setup_inputs_small(rng):
    d = setup_inputs(rng)
    for k in ("x", "w"): d[k] = (d[k].astype(np.float32) * (1 / 1024.0)).astype(d[k].dtype)
    return d
def setup_inputs_apart(rng):
    d = setup_inputs(rng)
    f = (10.0 ** rng.permutation(np.linspace(-1.5, 1.5, N))).astype(np.float32).reshape(N, 1, 1)
    for k in ("x", "w"): d[k] = (d[k].astype(np.float32) * f).astype(d[k].dtype)
    return d
def tie_inputs(x):
    x = dict(x)
    x["x"] = np.concatenate([x["x"][:NT], x["x"][:NT]])
    return x
def reference(x, w):
    X, W = x.astype(np.float64), w.astype(np.float64)
    y = np.stack([sum(W[r][:, 128 * j:128 * j + 128].T @ X[j if r < NT else j + NT] for j in range(NT)) for r in range(N)])
    return {"y": y.astype(ml_dtypes.bfloat16 if x.dtype != np.float64 else np.float64)}

from concourse.bass import DstId, RemoteDMATransfer

NT, TK, M = 4, 256, 128

SCRATCH = {
    "xs": ("sbuf", [128, NT * TK], "bfloat16"),
    "ws": ("sbuf", [128, NT * M], "bfloat16"),
    "acc": ("psum", [128, TK], "float32"),
    "ys": ("sbuf", [128, TK], "bfloat16"),
}
SEMAPHORES = ["xl", "wl", "sent", "a0", "a1", "a2", "a3", "mm", "cp", "st"]


def _source(T, topo, q, j):
    for s in (j, j + NT):
        if topo.same_plane(T.cores[s], T.cores[q]) and topo.may_write(T.cores[s], T.cores[q]):
            return s
    return None


def rank_program(g, core, T, topo):
    r = T.rank_of(core)
    if r is None:
        return
    own = r % NT
    slot = lambda j: T.xs[:, j * TK:(j + 1) * TK]
    tile = lambda j: T.ws[:, j * M:(j + 1) * M]

    g.sync.dma_start(slot(own), T.x[:]).then_inc(T.sem.xl, 16)
    g.sync.dma_start(T.ws[:], T.w[:]).then_inc(T.sem.wl, 16)

    takers = [q for q in range(len(T.cores)) if q != r and q % NT != own and _source(T, topo, q, own) == r]
    takers.sort(key=lambda q: (q - r) % NT)
    mask = topo.mask(core, T.cores[takers[0]])
    ids = []
    for q in takers:
        mask &= topo.mask(core, T.cores[q])
        rid, pid = topo.addr(T.cores[q], core)
        ids.append(DstId(rid=rid, pnc=pid))
    engines = bin(mask).count("1")
    g.wait_ge(T.sem.xl, 16)
    g.remote_dma_fused(
        [RemoteDMATransfer(dst_ids=ids, dma_engine_mask=mask, remote_sem=T.sem["a%d" % own],
                           src=slot(own), dsts=[slot(own) for _ in takers])],
        local_sem=T.sem.sent)

    g.tensor.wait_ge(T.sem.xl, 16)
    g.tensor.wait_ge(T.sem.wl, 16)
    g.tensor.matmul(T.acc[:], tile(own), slot(own), start=True, stop=False)
    for k in range(1, NT):
        j = (own - k) % NT
        src = T.cores[_source(T, topo, r, j)]
        g.tensor.wait_ge(T.sem["a%d" % j], bin(topo.mask(src, core)).count("1"))
        mm = g.tensor.matmul(T.acc[:], tile(j), slot(j), start=False, stop=(k == NT - 1))
    mm.then_inc(T.sem.mm, 1)

    g.vector.wait_ge(T.sem.mm, 1)
    g.vector.tensor_copy(T.ys[:], T.acc[:]).then_inc(T.sem.cp, 1)
    g.sync.wait_ge(T.sem.cp, 1)
    g.sync.dma_start(T.y[:], T.ys[:]).then_inc(T.sem.st, 16)

    g.wait_ge(T.sem.sent, engines)
    g.wait_ge(T.sem.st, 16)
